import numpy as np
import ml_dtypes

BF16 = ml_dtypes.bfloat16


def bf(x):
    return np.asarray(x, np.float32).astype(BF16)


def f32(x):
    return np.asarray(x, np.float32)


def f64(x):
    return np.asarray(x).astype(np.float64)


def striped(idx):
    return np.tile(idx.reshape(-1, 16).T, (8, 1))


S, K, M, N = 1024, 128, 128, 256


def setup_inputs():
    return {"table": bf(np.random.standard_normal((S, K))), "w": bf(np.random.standard_normal((K, M)) / np.sqrt(K)), "s": f32(0.5 + np.random.random_sample((M, 1))), "b": f32(0.5 * np.random.standard_normal((M, 1))), "offs": striped(np.sort(np.random.permutation(S)[:N]))}


def reference(table, w, s, b, offs):
    idx = offs[:16].T.reshape(-1)
    x = f64(table)[idx].T
    y = f64(w).T @ x
    return y * f64(s) + f64(b)

@@ -1,0 +1,83 @@
+import concourse.mybir as mybir
+from concourse.masks import make_identity
+
+S, K, M, N = 1024, 128, 128, 256
+P = 128
+BLOCKS_IN_PIECE = 2
+PIECES = S // (P * BLOCKS_IN_PIECE)
+PIECE_TOKENS = P * BLOCKS_IN_PIECE
+
+HALVES = 2
+HALF = N // HALVES
+WARM_COLUMNS = 512
+WARM_MATMULS = 3
+
+FLOPS = 2 * K * M * N
+
+BF16, F32, U16 = mybir.dt.bfloat16, mybir.dt.float32, mybir.dt.uint16
+MULT, ADD = mybir.AluOpType.mult, mybir.AluOpType.add
+IDENTITY = mybir.ActivationFunctionType.Identity
+
+
+def tile_gather_matmul_kernel(tc, table, w, s, b, offs, out):
+    nc = tc.nc
+    with (
+        tc.tile_pool(name="held", bufs=1) as held,
+        tc.psum_pool(name="flipped", bufs=PIECES) as flipped,
+        tc.psum_pool(name="product", bufs=1) as product,
+    ):
+        zeros = held.tile([P, WARM_COLUMNS], BF16, name="zeros")
+        nc.vector.memset(zeros[:], 0.0)
+        unread = product.tile([P, WARM_COLUMNS], F32, name="unread")
+        for warm in range(WARM_MATMULS):
+            nc.tensor.matmul(unread[:], zeros[:, 0:P], zeros[:], start=True, stop=True)
+
+        pieces_in_hbm = table.rearrange("(g p a) k -> g p a k", p=P, a=BLOCKS_IN_PIECE)
+        token_rows = []
+        for piece in range(PIECES):
+            rows = held.tile([P, BLOCKS_IN_PIECE, K], BF16, name="rows%d" % piece)
+            queue = nc.sync if piece % 2 == 0 else nc.scalar
+            queue.dma_start(rows[:], pieces_in_hbm[piece])
+            token_rows.append(rows)
+
+        offsets = held.tile([P, N // 16], U16, name="offsets")
+        nc.sync.dma_start(offsets[:], offs)
+        weights = held.tile([K, M], BF16, name="weights")
+        nc.scalar.dma_start(weights[:], w)
+        gain = held.tile([M, 1], F32, name="gain")
+        nc.sync.dma_start(gain[:], s)
+        shift = held.tile([M, 1], F32, name="shift")
+        nc.scalar.dma_start(shift[:], b)
+
+        identity = held.tile([P, P], BF16, name="identity")
+        make_identity(nc, identity[:])
+
+        window = held.tile([K, S], BF16, name="window")
+        for piece in range(PIECES):
+            flip = flipped.tile([K, PIECE_TOKENS], BF16, name="flip")
+            for block in range(BLOCKS_IN_PIECE):
+                nc.tensor.transpose(
+                    flip[:, block * P : (block + 1) * P],
+                    token_rows[piece][:, block, :],
+                    identity[:],
+                )
+            columns = window[:, piece * PIECE_TOKENS : (piece + 1) * PIECE_TOKENS]
+            columns = columns.rearrange("k (p a) -> k p a", a=BLOCKS_IN_PIECE)
+            in_turn = flip[:].rearrange("k (a p) -> k p a", a=BLOCKS_IN_PIECE)
+            if piece % 2 == 0:
+                nc.vector.tensor_copy(columns, in_turn)
+            else:
+                nc.scalar.copy(columns, in_turn)
+
+        for half in range(HALVES):
+            y = product.tile([M, HALF], F32, name="y%d" % half)
+            picked = window[:].indirect(offsets[:, half * HALF // 16 : (half + 1) * HALF // 16])
+            nc.tensor.matmul(y[:], weights[:], picked, start=True, stop=True)
+            result = held.tile([M, HALF], F32, name="result%d" % half)
+            out_columns = out[:, half * HALF : (half + 1) * HALF]
+            if half == 0:
+                nc.vector.tensor_scalar(result[:], y[:], gain[:, 0:1], shift[:, 0:1], MULT, ADD)
+                nc.sync.dma_start(out_columns, result[:])
+            else:
+                nc.scalar.activation(result[:], y[:], IDENTITY, bias=shift[:, 0:1], scale=gain[:, 0:1])
+                nc.scalar.dma_start(out_columns, result[:])

@@ -36,8 +36,7 @@ def tile_gather_matmul_kernel(tc, table, w, s, b, offs, out):
         token_rows = []
         for piece in range(PIECES):
             rows = held.tile([P, BLOCKS_IN_PIECE, K], BF16, name="rows%d" % piece)
-            queue = nc.sync if piece % 2 == 0 else nc.scalar
-            queue.dma_start(rows[:], pieces_in_hbm[piece])
+            nc.sync.dma_start(rows[:], pieces_in_hbm[piece])
             token_rows.append(rows)
 
         offsets = held.tile([P, N // 16], U16, name="offsets")
@@ -45,7 +44,7 @@ def tile_gather_matmul_kernel(tc, table, w, s, b, offs, out):
         weights = held.tile([K, M], BF16, name="weights")
         nc.scalar.dma_start(weights[:], w)
         gain = held.tile([M, 1], F32, name="gain")
-        nc.sync.dma_start(gain[:], s)
+        nc.scalar.dma_start(gain[:], s)
         shift = held.tile([M, 1], F32, name="shift")
         nc.scalar.dma_start(shift[:], b)
 

@@ -68,15 +68,14 @@ def tile_gather_matmul_kernel(tc, table, w, s, b, offs, out):
             else:
                 nc.scalar.copy(columns, in_turn)
 
+        result = held.tile([M, N], F32, name="result")
         for half in range(HALVES):
             y = product.tile([M, HALF], F32, name="y%d" % half)
             picked = window[:].indirect(offsets[:, half * HALF // 16 : (half + 1) * HALF // 16])
             nc.tensor.matmul(y[:], weights[:], picked, start=True, stop=True)
-            result = held.tile([M, HALF], F32, name="result%d" % half)
-            out_columns = out[:, half * HALF : (half + 1) * HALF]
+            result_columns = result[:, half * HALF : (half + 1) * HALF]
             if half == 0:
-                nc.vector.tensor_scalar(result[:], y[:], gain[:, 0:1], shift[:, 0:1], MULT, ADD)
-                nc.sync.dma_start(out_columns, result[:])
+                nc.vector.tensor_scalar(result_columns, y[:], gain[:, 0:1], shift[:, 0:1], MULT, ADD)
             else:
-                nc.scalar.activation(result[:], y[:], IDENTITY, bias=shift[:, 0:1], scale=gain[:, 0:1])
-                nc.scalar.dma_start(out_columns, result[:])
+                nc.scalar.activation(result_columns, y[:], IDENTITY, bias=shift[:, 0:1], scale=gain[:, 0:1])
+        nc.sync.dma_start(out, result[:])

@@ -36,7 +36,8 @@ def tile_gather_matmul_kernel(tc, table, w, s, b, offs, out):
         token_rows = []
         for piece in range(PIECES):
             rows = held.tile([P, BLOCKS_IN_PIECE, K], BF16, name="rows%d" % piece)
-            nc.sync.dma_start(rows[:], pieces_in_hbm[piece])
+            queue = nc.scalar if piece == 1 else nc.sync
+            queue.dma_start(rows[:], pieces_in_hbm[piece])
             token_rows.append(rows)
 
         offsets = held.tile([P, N // 16], U16, name="offsets")

@@ -47,7 +47,7 @@ def tile_gather_matmul_kernel(tc, table, w, s, b, offs, out):
         gain = held.tile([M, 1], F32, name="gain")
         nc.scalar.dma_start(gain[:], s)
         shift = held.tile([M, 1], F32, name="shift")
-        nc.scalar.dma_start(shift[:], b)
+        nc.sync.dma_start(shift[:], b)
 
         identity = held.tile([P, P], BF16, name="identity")
         make_identity(nc, identity[:])

@@ -32,13 +32,16 @@ def tile_gather_matmul_kernel(tc, table, w, s, b, offs, out):
         for warm in range(WARM_MATMULS):
             nc.tensor.matmul(unread[:], zeros[:, 0:P], zeros[:], start=True, stop=True)
 
-        pieces_in_hbm = table.rearrange("(g p a) k -> g p a k", p=P, a=BLOCKS_IN_PIECE)
-        token_rows = []
-        for piece in range(PIECES):
-            rows = held.tile([P, BLOCKS_IN_PIECE, K], BF16, name="rows%d" % piece)
-            queue = nc.scalar if piece == 1 else nc.sync
-            queue.dma_start(rows[:], pieces_in_hbm[piece])
-            token_rows.append(rows)
+        pieces_in_hbm = table.rearrange("(g p a) k -> p g a k", p=P, a=BLOCKS_IN_PIECE)
+        first_rows = held.tile([P, BLOCKS_IN_PIECE, K], BF16, name="first_rows")
+        second_rows = held.tile([P, BLOCKS_IN_PIECE, K], BF16, name="second_rows")
+        other_rows = held.tile([P, PIECES - 2, BLOCKS_IN_PIECE, K], BF16, name="other_rows")
+        nc.sync.dma_start(first_rows[:], pieces_in_hbm[:, 0])
+        nc.scalar.dma_start(second_rows[:], pieces_in_hbm[:, 1])
+        nc.sync.dma_start(other_rows[:], pieces_in_hbm[:, 2:PIECES])
+        token_rows = [first_rows[:], second_rows[:]]
+        for other in range(PIECES - 2):
+            token_rows.append(other_rows[:, other])
 
         offsets = held.tile([P, N // 16], U16, name="offsets")
         nc.sync.dma_start(offsets[:], offs)
@@ -58,7 +61,7 @@ def tile_gather_matmul_kernel(tc, table, w, s, b, offs, out):
             for block in range(BLOCKS_IN_PIECE):
                 nc.tensor.transpose(
                     flip[:, block * P : (block + 1) * P],
-                    token_rows[piece][:, block, :],
+                    token_rows[piece][:, block],
                     identity[:],
                 )
             columns = window[:, piece * PIECE_TOKENS : (piece + 1) * PIECE_TOKENS]

@@ -33,15 +33,14 @@ def tile_gather_matmul_kernel(tc, table, w, s, b, offs, out):
             nc.tensor.matmul(unread[:], zeros[:, 0:P], zeros[:], start=True, stop=True)
 
         pieces_in_hbm = table.rearrange("(g p a) k -> p g a k", p=P, a=BLOCKS_IN_PIECE)
-        first_rows = held.tile([P, BLOCKS_IN_PIECE, K], BF16, name="first_rows")
-        second_rows = held.tile([P, BLOCKS_IN_PIECE, K], BF16, name="second_rows")
-        other_rows = held.tile([P, PIECES - 2, BLOCKS_IN_PIECE, K], BF16, name="other_rows")
-        nc.sync.dma_start(first_rows[:], pieces_in_hbm[:, 0])
-        nc.scalar.dma_start(second_rows[:], pieces_in_hbm[:, 1])
-        nc.sync.dma_start(other_rows[:], pieces_in_hbm[:, 2:PIECES])
-        token_rows = [first_rows[:], second_rows[:]]
-        for other in range(PIECES - 2):
-            token_rows.append(other_rows[:, other])
+        lower_rows = held.tile([P, PIECES // 2, BLOCKS_IN_PIECE, K], BF16, name="lower_rows")
+        upper_rows = held.tile([P, PIECES // 2, BLOCKS_IN_PIECE, K], BF16, name="upper_rows")
+        nc.sync.dma_start(lower_rows[:], pieces_in_hbm[:, 0 : PIECES // 2])
+        nc.scalar.dma_start(upper_rows[:], pieces_in_hbm[:, PIECES // 2 : PIECES])
+        token_rows = []
+        for rows in (lower_rows, upper_rows):
+            for piece in range(PIECES // 2):
+                token_rows.append(rows[:, piece])
 
         offsets = held.tile([P, N // 16], U16, name="offsets")
         nc.sync.dma_start(offsets[:], offs)

@@ -71,14 +71,15 @@ def tile_gather_matmul_kernel(tc, table, w, s, b, offs, out):
             else:
                 nc.scalar.copy(columns, in_turn)
 
-        result = held.tile([M, N], F32, name="result")
         for half in range(HALVES):
             y = product.tile([M, HALF], F32, name="y%d" % half)
             picked = window[:].indirect(offsets[:, half * HALF // 16 : (half + 1) * HALF // 16])
             nc.tensor.matmul(y[:], weights[:], picked, start=True, stop=True)
-            result_columns = result[:, half * HALF : (half + 1) * HALF]
+            result = held.tile([M, HALF], F32, name="result%d" % half)
+            out_columns = out[:, half * HALF : (half + 1) * HALF]
             if half == 0:
-                nc.vector.tensor_scalar(result_columns, y[:], gain[:, 0:1], shift[:, 0:1], MULT, ADD)
+                nc.vector.tensor_scalar(result[:], y[:], gain[:, 0:1], shift[:, 0:1], MULT, ADD)
+                nc.sync.dma_start(out_columns, result[:])
             else:
-                nc.scalar.activation(result_columns, y[:], IDENTITY, bias=shift[:, 0:1], scale=gain[:, 0:1])
-        nc.sync.dma_start(out, result[:])
+                nc.scalar.activation(result[:], y[:], IDENTITY, bias=shift[:, 0:1], scale=gain[:, 0:1])
+                nc.scalar.dma_start(out_columns, result[:])

import concourse.mybir as mybir
from concourse.masks import make_identity

S, K, M, N = 1024, 128, 128, 256
P = 128
BLOCKS_IN_PIECE = 2
PIECES = S // (P * BLOCKS_IN_PIECE)
PIECE_TOKENS = P * BLOCKS_IN_PIECE

HALVES = 2
HALF = N // HALVES
WARM_COLUMNS = 512
WARM_MATMULS = 3

FLOPS = 2 * K * M * N

BF16, F32, U16 = mybir.dt.bfloat16, mybir.dt.float32, mybir.dt.uint16
MULT, ADD = mybir.AluOpType.mult, mybir.AluOpType.add
IDENTITY = mybir.ActivationFunctionType.Identity


def tile_gather_matmul_kernel(tc, table, w, s, b, offs, out):
    nc = tc.nc
    with (
        tc.tile_pool(name="held", bufs=1) as held,
        tc.psum_pool(name="flipped", bufs=PIECES) as flipped,
        tc.psum_pool(name="product", bufs=1) as product,
    ):
        zeros = held.tile([P, WARM_COLUMNS], BF16, name="zeros")
        nc.vector.memset(zeros[:], 0.0)
        unread = product.tile([P, WARM_COLUMNS], F32, name="unread")
        for warm in range(WARM_MATMULS):
            nc.tensor.matmul(unread[:], zeros[:, 0:P], zeros[:], start=True, stop=True)

        pieces_in_hbm = table.rearrange("(g p a) k -> p g a k", p=P, a=BLOCKS_IN_PIECE)
        lower_rows = held.tile([P, PIECES // 2, BLOCKS_IN_PIECE, K], BF16, name="lower_rows")
        upper_rows = held.tile([P, PIECES // 2, BLOCKS_IN_PIECE, K], BF16, name="upper_rows")
        nc.sync.dma_start(lower_rows[:], pieces_in_hbm[:, 0 : PIECES // 2])
        nc.scalar.dma_start(upper_rows[:], pieces_in_hbm[:, PIECES // 2 : PIECES])
        token_rows = []
        for rows in (lower_rows, upper_rows):
            for piece in range(PIECES // 2):
                token_rows.append(rows[:, piece])

        offsets = held.tile([P, N // 16], U16, name="offsets")
        nc.sync.dma_start(offsets[:], offs)
        weights = held.tile([K, M], BF16, name="weights")
        nc.scalar.dma_start(weights[:], w)
        gain = held.tile([M, 1], F32, name="gain")
        nc.scalar.dma_start(gain[:], s)
        shift = held.tile([M, 1], F32, name="shift")
        nc.sync.dma_start(shift[:], b)

        identity = held.tile([P, P], BF16, name="identity")
        make_identity(nc, identity[:])

        window = held.tile([K, S], BF16, name="window")
        for piece in range(PIECES):
            flip = flipped.tile([K, PIECE_TOKENS], BF16, name="flip")
            for block in range(BLOCKS_IN_PIECE):
                nc.tensor.transpose(
                    flip[:, block * P : (block + 1) * P],
                    token_rows[piece][:, block],
                    identity[:],
                )
            columns = window[:, piece * PIECE_TOKENS : (piece + 1) * PIECE_TOKENS]
            columns = columns.rearrange("k (p a) -> k p a", a=BLOCKS_IN_PIECE)
            in_turn = flip[:].rearrange("k (a p) -> k p a", a=BLOCKS_IN_PIECE)
            if piece % 2 == 0:
                nc.vector.tensor_copy(columns, in_turn)
            else:
                nc.scalar.copy(columns, in_turn)

        for half in range(HALVES):
            y = product.tile([M, HALF], F32, name="y%d" % half)
            picked = window[:].indirect(offsets[:, half * HALF // 16 : (half + 1) * HALF // 16])
            nc.tensor.matmul(y[:], weights[:], picked, start=True, stop=True)
            result = held.tile([M, HALF], F32, name="result%d" % half)
            out_columns = out[:, half * HALF : (half + 1) * HALF]
            if half == 0:
                nc.vector.tensor_scalar(result[:], y[:], gain[:, 0:1], shift[:, 0:1], MULT, ADD)
                nc.sync.dma_start(out_columns, result[:])
            else:
                nc.scalar.activation(result[:], y[:], IDENTITY, bias=shift[:, 0:1], scale=gain[:, 0:1])
                nc.scalar.dma_start(out_columns, result[:])
